import numpy as np
import ml_dtypes


def mxq(x, axis, fmt="e4m3"):
    dtype, down = {"e4m3": (ml_dtypes.float8_e4m3fn, 7), "e5m2": (ml_dtypes.float8_e5m2, 14)}[fmt]
    v = np.moveaxis(np.asarray(x, np.float32).astype(ml_dtypes.bfloat16).astype(np.float64), axis, -1)
    blocks = v.reshape(v.shape[:-1] + (-1, 32))
    amax = np.abs(blocks).max(-1, keepdims=True)
    byte = np.maximum(np.where(amax > 0, np.frexp(amax)[1] - 1 + 127, 0) - down, 1)
    scale = np.exp2(byte - 127.0)
    codes = (blocks / scale).astype(np.float32).astype(dtype).astype(np.float64)
    return np.moveaxis((codes * scale).reshape(v.shape), -1, axis)


WIDE = False


def mx_kscale(k):
    if not WIDE:
        return np.ones(k)
    levels = np.array([10, -10, 5, -5, 0])
    if k % 512:
        return np.exp2(np.random.permutation(np.resize(levels, k // 32))).repeat(32)
    a = np.empty((k // 512, 16))
    for p in range(k // 512):
        a[p, :8] = np.random.permutation(np.resize(levels, 8))
        for g in range(8):
            far = levels[np.abs(levels - a[p, g]) >= 10]
            a[p, g + 8] = far[np.random.randint(len(far))]
    return np.exp2(a.ravel()).repeat(32)


def f64(x):
    return np.asarray(x).astype(np.float64)


def striped(idx):
    return np.tile(np.asarray(idx).reshape(-1, 16).T, (8, 1)).astype(np.uint16)


def unstriped(offs):
    return offs[:16].T.reshape(-1).astype(np.int64)


E2M1 = np.array([0.0, 0.5, 1.0, 1.5, 2.0, 3.0, 4.0, 6.0, -0.0, -0.5, -1.0, -1.5, -2.0, -3.0, -4.0, -6.0])


def pack_weight(w, fmt):
    k, n = w.shape
    w = f64(np.asarray(w, np.float32).astype(ml_dtypes.bfloat16)).reshape(k // 32, 32, n)
    amax = np.abs(w).max(1)
    if fmt == "e4m3":
        byte = np.frexp(amax)[1] - 1 + 127 - 7
    else:
        mant, ex = np.frexp(amax / 6.0)
        byte = np.where(mant > 0.5, ex, ex - 1) + 127
    byte = np.clip(np.where(amax > 0, byte, 1), 1, 254)
    scaled = (w * np.exp2(127.0 - byte)[:, None, :]).reshape(k, n).astype(np.float32)
    by_word = np.ascontiguousarray(scaled.reshape(k // 512, 128, 4, n).transpose(0, 1, 3, 2))
    if fmt == "e4m3":
        words = by_word.astype(ml_dtypes.float8_e4m3fn).view(np.uint8)
    else:
        c = by_word.astype(ml_dtypes.float4_e2m1fn).view(np.uint8) & 0xF
        words = (c[..., 0::2] | (c[..., 1::2] << 4)).reshape(k // 512, 128, 2 * n)
    return np.ascontiguousarray(words), np.ascontiguousarray(byte.astype(np.uint8).reshape(k // 512, 16, n))


def unpack_weight(words, scales, fmt):
    g, _, n = scales.shape
    words = np.ascontiguousarray(words).reshape(g, 128, n, -1)
    if fmt == "e4m3":
        vals = words.view(ml_dtypes.float8_e4m3fn).astype(np.float64)
    else:
        nib = np.empty((g, 128, n, 4), np.uint8)
        nib[..., 0::2] = words & 0xF
        nib[..., 1::2] = words >> 4
        vals = E2M1[nib]
    vals = vals * np.repeat(np.exp2(scales.astype(np.float64) - 127.0), 8, axis=1)[..., None]
    return vals.transpose(0, 1, 3, 2).reshape(g * 512, n)


def bf(x):
    return np.asarray(x, np.float32).astype(ml_dtypes.bfloat16)


def planes(Y):
    r, m = Y.shape
    b = f64(bf(Y)).reshape(r // 32, 32, m)
    amax = np.abs(b).max(1)
    byte = np.clip(np.where(amax > 0, np.frexp(amax)[1] - 1 + 127 - 7, 1), 1, 254)
    codes = (b * np.exp2(127.0 - byte)[:, None, :]).reshape(r, m).astype(np.float32).astype(ml_dtypes.float8_e4m3fn).view(np.uint8)
    words = codes.reshape(r // 512, 128, 4, m).transpose(0, 1, 3, 2)
    return np.ascontiguousarray(words), np.ascontiguousarray(byte.astype(np.uint8).reshape(r // 512, 16, m))


D, T, I, J, U, E = 512, 2048, 512, 512, 1024, 512


def setup_inputs():
    n = np.random.standard_normal
    idx = np.random.permutation(T)[:I]
    idx2 = np.random.permutation(U)[:J]
    idx3 = np.random.permutation(U)[:J]
    fd = mx_kscale(D)
    fi = mx_kscale(I)
    ti = np.ones(T)
    ti[idx] = fi
    keysp = pack_weight(n((D, T)) / fd[:, None], "e2m1")
    return {
        "keys_words": keysp[0],
        "keys_scales": keysp[1],
        "notes": (n((D, U)) * 1.0 / np.sqrt(D) * fd[:, None]).astype(np.float32),
        "rowf": (np.random.uniform(0.02, 0.08, (I, 1)) * fi[:, None]).astype(np.float32),
        "vals": (n((E, T)) / ti).astype(np.float32),
        "mem": (np.random.uniform(0.3, 1.0, (1, J))).astype(np.float32),
        "offs": striped(idx),
        "offs2": striped(idx2),
        "offs3": striped(idx3),
    }


def reference(keys_words, keys_scales, notes, rowf, vals, mem, offs, offs2, offs3):
    idx = unstriped(offs)
    idx2 = unstriped(offs2)
    idx3 = unstriped(offs3)
    keysu = unpack_weight(keys_words, keys_scales, "e2m1")
    keysidxg = keysu[:, idx]
    notesq = mxq(f64(notes), 0, "e4m3")
    g1 = keysidxg.T @ notesq
    g9 = g1[:, idx2] - g1[:, idx3]
    g0 = np.maximum(g9, 0.0)
    gr1 = g0 * f64(rowf)
    vt1 = f64(vals)[:, idx].T
    vt1q = mxq(vt1, 0, "e4m3")
    gr1q = mxq(gr1, 0, "e4m3")
    o = vt1q.T @ gr1q
    o1 = np.pad(o, ((0, 0), (1, 0)))[:, :J]
    y = o - o1 * f64(mem)
    words, scales = planes(y)
    return y, words, scales

@@ -1,0 +1,223 @@
+from contextlib import ExitStack
+
+import concourse.mybir as mybir
+from concourse.masks import make_identity
+
+F32 = mybir.dt.float32
+BF16 = mybir.dt.bfloat16
+I32 = mybir.dt.int32
+U32 = mybir.dt.uint32
+U16 = mybir.dt.uint16
+U8 = mybir.dt.uint8
+FP8X4 = mybir.dt.float8_e4m3fn_x4
+FP4X4 = mybir.dt.float4_e2m1fn_x4
+ALU = mybir.AluOpType
+COPY = mybir.ActivationFunctionType.Copy
+
+P = 128
+D, T, I, J, U, E = 512, 2048, 512, 512, 1024, 512
+FLOPS = 2 * D * I * U + 2 * I * E * J
+NC = 4
+CW = U // NC
+JH = J // 2
+PAD = 8
+
+
+def tile_attend_tab_looked_changes_pl_kernel(tc, keys_words, keys_scales, notes, rowf, vals, mem, offs, offs2, offs3, out_0, out_1, out_2):
+    nc = tc.nc
+    with ExitStack() as ctx:
+        sb = ctx.enter_context(tc.tile_pool(name="sb", bufs=1))
+        acc_pool = ctx.enter_context(tc.psum_pool(name="acc", bufs=6))
+        turn_pool = ctx.enter_context(tc.psum_pool(name="turn", bufs=2))
+
+        def tile(shape, dtype, name, tag=None):
+            return sb.tile(shape, dtype, name=name, tag=tag or name, align_bytes=64)
+
+        o1 = tile([P, 32], U16, "o1")
+        o2 = tile([P, 32], U16, "o2")
+        o3 = tile([P, 32], U16, "o3")
+        kw = tile([P, T], U16, "kw")
+        ks = tile([P, T], U8, "ks")
+        nraw = [tile([P, 4, CW], F32, "nraw%d" % c) for c in range(NC)]
+        vraw = [tile([P, T], F32, "vraw%d" % r) for r in range(4)]
+        rf = tile([P, 4], F32, "rf")
+        mb = tile([P, J], F32, "mb")
+        tmp = tile([P, 4, PAD + J], F32, "tmp")
+        ident = tile([P, P], F32, "ident")
+
+        nc.vector.memset(ks[:].bitcast(I32), 0)
+        nc.vector.memset(tmp[:, :, PAD - 1 : PAD], 0.0)
+        make_identity(nc, ident[:])
+
+        nc.sync.dma_start(o1[:], offs)
+        nc.sync.dma_start(kw[:].bitcast(I32), keys_words[0].bitcast(I32))
+        for q in range(4):
+            nc.sync.dma_start(ks[32 * q : 32 * q + 4, :].bitcast(I32), keys_scales[0, 4 * q : 4 * q + 4, :].bitcast(I32))
+        nview = notes.rearrange("(p t) u -> p t u", t=4)
+        for c in range(NC):
+            nc.sync.dma_start(nraw[c][:], nview[:, :, c * CW : (c + 1) * CW])
+        nc.sync.dma_start(o2[:], offs2)
+        nc.sync.dma_start(o3[:], offs3)
+        nc.sync.dma_start(rf[:], rowf.rearrange("(p t) o -> p (t o)", t=4))
+        vview = vals.rearrange("(m r) t -> r m t", r=4)
+        for r in range(4):
+            nc.sync.dma_start(vraw[r][:], vview[r])
+            if r == 1:
+                nc.sync.dma_start(mb[:], mem[0].partition_broadcast(P))
+
+        kg = tile([P, I], U16, "kg")
+        kd = tile([P, I], U16, "kd")
+        ksd = tile([P, I], U8, "ksd")
+        nc.vector.tensor_copy(kg[:], kw[:].indirect(o1[:]))
+        nc.vector.tensor_copy(ksd[:].rearrange("p (t m) -> p m t", t=4), ks[:].indirect(o1[:]))
+        nc.vector.tensor_copy(kd[:].rearrange("p (t m) -> p t m", t=4), kg[:].rearrange("p (m t) -> p t m", t=4))
+
+        ncode = tile([P, U], U32, "ncode")
+        nscale = tile([P, U], U8, "nscale")
+        nb = [tile([P, CW, 4], BF16, "nb%d" % c) for c in range(NC)]
+
+        def weave(dst, src):
+            return dst.rearrange("p (c i) t -> p c t i", i=4), src.rearrange("p t (c i) -> p c t i", i=4)
+
+        def cast_notes(c):
+            dst, src = weave(nb[c][:], nraw[c][:])
+            if c < 3:
+                nc.scalar.activation(dst, src, COPY)
+            else:
+                nc.vector.tensor_copy(dst, src)
+
+        def quant_notes(c):
+            cols = slice(c * CW, (c + 1) * CW)
+            nc.vector.quantize_mx(out=ncode[:, cols].bitcast(FP8X4), scales=nscale[:, cols], in_=nb[c][:].rearrange("p c t -> p (c t)"))
+
+        g1 = [tile([P, U], F32, "g1_%d" % t) for t in range(4)]
+
+        banks = {}
+
+        def wide(t, lo, hi):
+            h = lo // 512
+            if lo % 512 == 0:
+                banks[t, h] = acc_pool.tile([P, 512], F32, name="acc")
+            rows = slice(t * P, (t + 1) * P)
+            nc.tensor.matmul_mx(out=banks[t, h][:, lo - h * 512 : hi - h * 512], lhsT=kd[:, rows].bitcast(FP4X4), lhsT_scale=ksd[:, rows],
+                                rhs=ncode[:, lo:hi].bitcast(FP8X4), rhs_scale=nscale[:, lo:hi], start=True, stop=True)
+
+        def empty(t, h):
+            dst = g1[t][:, h * 512 : (h + 1) * 512]
+            if h == 1 and t < 2:
+                nc.vector.tensor_copy(dst, banks[t, h][:])
+            else:
+                nc.scalar.copy(dst, banks[t, h][:])
+
+        for c in range(NC):
+            cast_notes(c)
+            quant_notes(c)
+            if c < 2:
+                for t in range(4):
+                    wide(t, c * CW, (c + 1) * CW)
+                    if c == 1:
+                        empty(t, 0)
+        for t in range(4):
+            wide(t, 512, U)
+        for t in range(2):
+            empty(t, 1)
+
+        gb = [tile([P, J], F32, "gb%d" % t) for t in range(4)]
+        g9 = [tile([P, J], F32, "g9_%d" % t) for t in range(4)]
+        gr = tile([P, 4, J], BF16, "gr")
+        vg = [tile([P, I], BF16, "vg%d" % r) for r in range(4)]
+        vt = []
+        vcode = tile([P, E], U32, "vcode")
+        vscale = tile([P, E], U8, "vscale")
+
+        def table(t):
+            nc.scalar.activation(gb[t][:], g1[t][:].indirect(o3[:]), COPY)
+            nc.vector.tensor_tensor(g9[t][:], g1[t][:].indirect(o2[:]), gb[t][:], ALU.subtract)
+
+        def relu(t):
+            nc.vector.tensor_scalar(gr[:, t, :], g9[t][:], 0.0, rf[:, t : t + 1], ALU.max, ALU.mult)
+
+        turned = []
+
+        def values(r):
+            nc.scalar.activation(vg[r][:], vraw[r][:].indirect(o1[:]), COPY)
+            words = vg[r][:].bitcast(F32)
+            ps = turn_pool.tile([P, 2, P], F32, name="ps")
+            for u in range(2):
+                nc.tensor.transpose(ps[:, u, :], words[:, u : 2 * P : 2], ident[:])
+            turned.append(ps)
+
+        def empty_values(r):
+            ps = turned[r]
+            vt.append(tile([P, P, 4], BF16, "vt%d" % r, "vraw%d" % (r + 1)))
+            nc.scalar.copy(vt[r][:].rearrange("p e t -> p (e t)").bitcast(F32).rearrange("p (e u) -> p e u", u=2), ps[:].rearrange("p u e -> p e u"))
+
+        def quant_values(r):
+            cols = slice(r * P, (r + 1) * P)
+            nc.vector.quantize_mx(out=vcode[:, cols].bitcast(FP8X4), scales=vscale[:, cols], in_=vt[r][:].rearrange("p e t -> p (e t)"))
+
+        for t in range(4):
+            if t >= 2:
+                empty(t, 1)
+            table(t)
+            if t > 0:
+                relu(t - 1)
+        relu(3)
+        for r in range(4):
+            values(r)
+            if r > 0:
+                empty_values(r - 1)
+        empty_values(3)
+
+        gi = [tile([P, JH, 4], BF16, "gi%d" % h) for h in range(2)]
+        gcode = tile([P, J], U32, "gcode")
+        gscale = tile([P, J], U8, "gscale")
+        for h in range(2):
+            dst, src = weave(gi[h][:], gr[:, :, h * JH : (h + 1) * JH])
+            nc.vector.tensor_copy(dst, src)
+        for h in range(2):
+            cols = slice(h * JH, (h + 1) * JH)
+            nc.vector.quantize_mx(out=gcode[:, cols].bitcast(FP8X4), scales=gscale[:, cols], in_=gi[h][:].rearrange("p c t -> p (c t)"))
+
+        y = tile([P, 4, J], F32, "y")
+        yb = [tile([P, JH, 4], BF16, "yb%d" % h) for h in range(2)]
+        ycode = tile([P, J], U32, "ycode")
+        yscale = tile([P, J], U8, "yscale")
+        oview = out_0.rearrange("(p r) j -> p r j", r=4)
+        cview = out_1[0].rearrange("p c r -> p (c r)").bitcast(I32)
+
+        def product(r):
+            rows = slice(r * P, (r + 1) * P)
+            acc = acc_pool.tile([P, 512], F32, name="acc")
+            nc.tensor.matmul_mx(out=acc[:], lhsT=vcode[:, rows].bitcast(FP8X4), lhsT_scale=vscale[:, rows],
+                                rhs=gcode[:].bitcast(FP8X4), rhs_scale=gscale[:], start=True, stop=True)
+            return acc
+
+        def damp(r, acc):
+            nc.vector.tensor_tensor(tmp[:, r, PAD : PAD + J - 1], acc[:, 0 : J - 1], mb[:, 1:J], ALU.mult)
+
+        def finish(r, acc):
+            nc.vector.tensor_tensor(y[:, r, :], acc[:], tmp[:, r, PAD - 1 : PAD - 1 + J], ALU.subtract)
+            nc.sync.dma_start(oview[:, r, :], y[:, r, :])
+
+        accs = []
+        for r in range(4):
+            quant_values(r)
+            accs.append(product(r))
+            if r > 0:
+                finish(r - 1, accs[r - 1])
+            damp(r, accs[r])
+        finish(3, accs[3])
+        for h in range(2):
+            dst, src = weave(yb[h][:], y[:, :, h * JH : (h + 1) * JH])
+            if h == 0:
+                nc.vector.tensor_copy(dst, src)
+            else:
+                nc.scalar.copy(dst, src)
+        for h in range(2):
+            cols = slice(h * JH, (h + 1) * JH)
+            nc.vector.quantize_mx(out=ycode[:, cols].bitcast(FP8X4), scales=yscale[:, cols], in_=yb[h][:].rearrange("p c t -> p (c t)"))
+            nc.sync.dma_start(cview[:, cols], ycode[:, cols].bitcast(I32))
+        for q in range(4):
+            eng = nc.sync if q % 2 else nc.scalar
+            eng.dma_start(out_2[0, 4 * q : 4 * q + 4, :].bitcast(I32), yscale[32 * q : 32 * q + 4, :].bitcast(I32))

@@ -41,7 +41,7 @@ def tile_attend_tab_looked_changes_pl_kernel(tc, keys_words, keys_scales, notes,
         nraw = [tile([P, 4, CW], F32, "nraw%d" % c) for c in range(NC)]
         vraw = [tile([P, T], F32, "vraw%d" % r) for r in range(4)]
         rf = tile([P, 4], F32, "rf")
-        mb = tile([P, J], F32, "mb")
+        mc = tile([P, 4], F32, "mc")
         tmp = tile([P, 4, PAD + J], F32, "tmp")
         ident = tile([P, P], F32, "ident")
 
@@ -50,6 +50,7 @@ def tile_attend_tab_looked_changes_pl_kernel(tc, keys_words, keys_scales, notes,
         make_identity(nc, ident[:])
 
         nc.sync.dma_start(o1[:], offs)
+        nc.sync.dma_start(mc[:], mem[0].rearrange("(p c) -> p c", c=4))
         nc.sync.dma_start(kw[:].bitcast(I32), keys_words[0].bitcast(I32))
         for q in range(4):
             nc.sync.dma_start(ks[32 * q : 32 * q + 4, :].bitcast(I32), keys_scales[0, 4 * q : 4 * q + 4, :].bitcast(I32))
@@ -62,8 +63,10 @@ def tile_attend_tab_looked_changes_pl_kernel(tc, keys_words, keys_scales, notes,
         vview = vals.rearrange("(m r) t -> r m t", r=4)
         for r in range(4):
             nc.sync.dma_start(vraw[r][:], vview[r])
-            if r == 1:
-                nc.sync.dma_start(mb[:], mem[0].partition_broadcast(P))
+
+        spread = turn_pool.tile([P, 4, P], F32, name="ps")
+        for c in range(4):
+            nc.tensor.transpose(spread[:, c, :], mc[:, c : c + 1].to_broadcast([P, P]), ident[:])
 
         kg = tile([P, I], U16, "kg")
         kd = tile([P, I], U16, "kd")
@@ -90,7 +93,7 @@ def tile_attend_tab_looked_changes_pl_kernel(tc, keys_words, keys_scales, notes,
             cols = slice(c * CW, (c + 1) * CW)
             nc.vector.quantize_mx(out=ncode[:, cols].bitcast(FP8X4), scales=nscale[:, cols], in_=nb[c][:].rearrange("p c t -> p (c t)"))
 
-        g1 = [tile([P, U], F32, "g1_%d" % t) for t in range(4)]
+        g1 = {}
 
         banks = {}
 
@@ -103,8 +106,10 @@ def tile_attend_tab_looked_changes_pl_kernel(tc, keys_words, keys_scales, notes,
                                 rhs=ncode[:, lo:hi].bitcast(FP8X4), rhs_scale=nscale[:, lo:hi], start=True, stop=True)
 
         def empty(t, h):
+            if h == 0:
+                g1[t] = tile([P, U], F32, "g1_%d" % t, {2: "nraw3", 3: "nb3"}.get(t))
             dst = g1[t][:, h * 512 : (h + 1) * 512]
-            if h == 1 and t < 2:
+            if (t, h) in ((2, 0), (3, 0), (1, 1), (2, 1)):
                 nc.vector.tensor_copy(dst, banks[t, h][:])
             else:
                 nc.scalar.copy(dst, banks[t, h][:])
@@ -112,14 +117,19 @@ def tile_attend_tab_looked_changes_pl_kernel(tc, keys_words, keys_scales, notes,
         for c in range(NC):
             cast_notes(c)
             quant_notes(c)
+            if c == 1:
+                mb = tile([P, J], F32, "mb", "nraw1")
+                nc.vector.tensor_copy(mb[:].rearrange("p (n c) -> p n c", c=4), spread[:].rearrange("p c n -> p n c"))
             if c < 2:
                 for t in range(4):
                     wide(t, c * CW, (c + 1) * CW)
-                    if c == 1:
+                    if c == 1 and t < 2:
                         empty(t, 0)
+        for t in range(2, 4):
+            empty(t, 0)
         for t in range(4):
             wide(t, 512, U)
-        for t in range(2):
+        for t in range(3):
             empty(t, 1)
 
         gb = [tile([P, J], F32, "gb%d" % t) for t in range(4)]
@@ -142,32 +152,31 @@ def tile_attend_tab_looked_changes_pl_kernel(tc, keys_words, keys_scales, notes,
         def values(r):
             nc.scalar.activation(vg[r][:], vraw[r][:].indirect(o1[:]), COPY)
             words = vg[r][:].bitcast(F32)
-            ps = turn_pool.tile([P, 2, P], F32, name="ps")
+            if r % 2 == 0:
+                turned.append(turn_pool.tile([P, 2, 2, P], F32, name="ps"))
             for u in range(2):
-                nc.tensor.transpose(ps[:, u, :], words[:, u : 2 * P : 2], ident[:])
-            turned.append(ps)
+                nc.tensor.transpose(turned[r // 2][:, r % 2, u, :], words[:, u : 2 * P : 2], ident[:])
 
-        def empty_values(r):
-            ps = turned[r]
-            vt.append(tile([P, P, 4], BF16, "vt%d" % r, "vraw%d" % (r + 1)))
-            nc.scalar.copy(vt[r][:].rearrange("p e t -> p (e t)").bitcast(F32).rearrange("p (e u) -> p e u", u=2), ps[:].rearrange("p u e -> p e u"))
+        def empty_values(rp):
+            vt.append(tile([P, 2 * P, 4], BF16, "vt%d" % rp, ("vraw2", "y")[rp]))
+            nc.scalar.copy(vt[rp][:].rearrange("p e t -> p (e t)").bitcast(F32).rearrange("p (r e u) -> p r e u", r=2, u=2),
+                           turned[rp][:].rearrange("p r u e -> p r e u"))
 
-        def quant_values(r):
-            cols = slice(r * P, (r + 1) * P)
-            nc.vector.quantize_mx(out=vcode[:, cols].bitcast(FP8X4), scales=vscale[:, cols], in_=vt[r][:].rearrange("p e t -> p (e t)"))
+        def quant_values(rp):
+            cols = slice(rp * 2 * P, (rp + 1) * 2 * P)
+            nc.vector.quantize_mx(out=vcode[:, cols].bitcast(FP8X4), scales=vscale[:, cols], in_=vt[rp][:].rearrange("p e t -> p (e t)"))
 
         for t in range(4):
-            if t >= 2:
-                empty(t, 1)
+            if t == 1:
+                empty(3, 1)
             table(t)
             if t > 0:
                 relu(t - 1)
         relu(3)
         for r in range(4):
             values(r)
-            if r > 0:
-                empty_values(r - 1)
-        empty_values(3)
+            if r >= 2:
+                empty_values(r - 2)
 
         gi = [tile([P, JH, 4], BF16, "gi%d" % h) for h in range(2)]
         gcode = tile([P, J], U32, "gcode")
@@ -179,7 +188,6 @@ def tile_attend_tab_looked_changes_pl_kernel(tc, keys_words, keys_scales, notes,
             cols = slice(h * JH, (h + 1) * JH)
             nc.vector.quantize_mx(out=gcode[:, cols].bitcast(FP8X4), scales=gscale[:, cols], in_=gi[h][:].rearrange("p c t -> p (c t)"))
 
-        y = tile([P, 4, J], F32, "y")
         yb = [tile([P, JH, 4], BF16, "yb%d" % h) for h in range(2)]
         ycode = tile([P, J], U32, "ycode")
         yscale = tile([P, J], U8, "yscale")
@@ -200,13 +208,18 @@ def tile_attend_tab_looked_changes_pl_kernel(tc, keys_words, keys_scales, notes,
             nc.vector.tensor_tensor(y[:, r, :], acc[:], tmp[:, r, PAD - 1 : PAD - 1 + J], ALU.subtract)
             nc.sync.dma_start(oview[:, r, :], y[:, r, :])
 
-        accs = []
-        for r in range(4):
-            quant_values(r)
-            accs.append(product(r))
-            if r > 0:
-                finish(r - 1, accs[r - 1])
-            damp(r, accs[r])
+        quant_values(0)
+        accs = [product(0), product(1)]
+        damp(0, accs[0])
+        damp(1, accs[1])
+        quant_values(1)
+        accs.extend([product(2), product(3)])
+        y = tile([P, 4, J], F32, "y")
+        finish(0, accs[0])
+        finish(1, accs[1])
+        damp(2, accs[2])
+        damp(3, accs[3])
+        finish(2, accs[2])
         finish(3, accs[3])
         for h in range(2):
             dst, src = weave(yb[h][:], y[:, :, h * JH : (h + 1) * JH])

@@ -27,7 +27,7 @@ def tile_attend_tab_looked_changes_pl_kernel(tc, keys_words, keys_scales, notes,
     nc = tc.nc
     with ExitStack() as ctx:
         sb = ctx.enter_context(tc.tile_pool(name="sb", bufs=1))
-        acc_pool = ctx.enter_context(tc.psum_pool(name="acc", bufs=6))
+        acc_pool = ctx.enter_context(tc.psum_pool(name="acc", bufs=1))
         turn_pool = ctx.enter_context(tc.psum_pool(name="turn", bufs=2))
 
         def tile(shape, dtype, name, tag=None):
@@ -41,7 +41,7 @@ def tile_attend_tab_looked_changes_pl_kernel(tc, keys_words, keys_scales, notes,
         nraw = [tile([P, 4, CW], F32, "nraw%d" % c) for c in range(NC)]
         vraw = [tile([P, T], F32, "vraw%d" % r) for r in range(4)]
         rf = tile([P, 4], F32, "rf")
-        mc = tile([P, 4], F32, "mc")
+        mb = tile([P, J], F32, "mb")
         tmp = tile([P, 4, PAD + J], F32, "tmp")
         ident = tile([P, P], F32, "ident")
 
@@ -50,23 +50,21 @@ def tile_attend_tab_looked_changes_pl_kernel(tc, keys_words, keys_scales, notes,
         make_identity(nc, ident[:])
 
         nc.sync.dma_start(o1[:], offs)
-        nc.sync.dma_start(mc[:], mem[0].rearrange("(p c) -> p c", c=4))
         nc.sync.dma_start(kw[:].bitcast(I32), keys_words[0].bitcast(I32))
         for q in range(4):
             nc.sync.dma_start(ks[32 * q : 32 * q + 4, :].bitcast(I32), keys_scales[0, 4 * q : 4 * q + 4, :].bitcast(I32))
         nview = notes.rearrange("(p t) u -> p t u", t=4)
         for c in range(NC):
             nc.sync.dma_start(nraw[c][:], nview[:, :, c * CW : (c + 1) * CW])
-        nc.sync.dma_start(o2[:], offs2)
-        nc.sync.dma_start(o3[:], offs3)
+            if c == 1:
+                nc.sync.dma_start(o3[:], offs3)
+                nc.sync.dma_start(o2[:], offs2)
         nc.sync.dma_start(rf[:], rowf.rearrange("(p t) o -> p (t o)", t=4))
         vview = vals.rearrange("(m r) t -> r m t", r=4)
         for r in range(4):
             nc.sync.dma_start(vraw[r][:], vview[r])
-
-        spread = turn_pool.tile([P, 4, P], F32, name="ps")
-        for c in range(4):
-            nc.tensor.transpose(spread[:, c, :], mc[:, c : c + 1].to_broadcast([P, P]), ident[:])
+            if r == 1:
+                nc.sync.dma_start(mb[:], mem[0].partition_broadcast(P))
 
         kg = tile([P, I], U16, "kg")
         kd = tile([P, I], U16, "kd")
@@ -77,20 +75,20 @@ def tile_attend_tab_looked_changes_pl_kernel(tc, keys_words, keys_scales, notes,
 
         ncode = tile([P, U], U32, "ncode")
         nscale = tile([P, U], U8, "nscale")
-        nb = [tile([P, CW, 4], BF16, "nb%d" % c) for c in range(NC)]
+        nb = [tile([P, CW, 4], BF16, "nb0"), tile([P, CW, 4], BF16, "nb1"), tile([P, 2 * CW, 4], BF16, "nb3")]
 
         def weave(dst, src):
             return dst.rearrange("p (c i) t -> p c t i", i=4), src.rearrange("p t (c i) -> p c t i", i=4)
 
         def cast_notes(c):
-            dst, src = weave(nb[c][:], nraw[c][:])
+            dst, src = weave(nb[c][:] if c < 2 else nb[2][:, (c - 2) * CW : (c - 1) * CW, :], nraw[c][:])
             if c < 3:
                 nc.scalar.activation(dst, src, COPY)
             else:
                 nc.vector.tensor_copy(dst, src)
 
         def quant_notes(c):
-            cols = slice(c * CW, (c + 1) * CW)
+            cols = slice(c * CW, (c + 1) * CW if c < 2 else U)
             nc.vector.quantize_mx(out=ncode[:, cols].bitcast(FP8X4), scales=nscale[:, cols], in_=nb[c][:].rearrange("p c t -> p (c t)"))
 
         g1 = {}
@@ -100,7 +98,7 @@ def tile_attend_tab_looked_changes_pl_kernel(tc, keys_words, keys_scales, notes,
         def wide(t, lo, hi):
             h = lo // 512
             if lo % 512 == 0:
-                banks[t, h] = acc_pool.tile([P, 512], F32, name="acc")
+                banks[t, h] = acc_pool.tile([P, 512], F32, name="acc", tag="bank%d" % ((0, 1, 2, 3), (4, 5, 0, 4))[h][t])
             rows = slice(t * P, (t + 1) * P)
             nc.tensor.matmul_mx(out=banks[t, h][:, lo - h * 512 : hi - h * 512], lhsT=kd[:, rows].bitcast(FP4X4), lhsT_scale=ksd[:, rows],
                                 rhs=ncode[:, lo:hi].bitcast(FP8X4), rhs_scale=nscale[:, lo:hi], start=True, stop=True)
@@ -116,10 +114,8 @@ def tile_attend_tab_looked_changes_pl_kernel(tc, keys_words, keys_scales, notes,
 
         for c in range(NC):
             cast_notes(c)
-            quant_notes(c)
-            if c == 1:
-                mb = tile([P, J], F32, "mb", "nraw1")
-                nc.vector.tensor_copy(mb[:].rearrange("p (n c) -> p n c", c=4), spread[:].rearrange("p c n -> p n c"))
+            if c != 2:
+                quant_notes(min(c, 2))
             if c < 2:
                 for t in range(4):
                     wide(t, c * CW, (c + 1) * CW)
@@ -196,7 +192,7 @@ def tile_attend_tab_looked_changes_pl_kernel(tc, keys_words, keys_scales, notes,
 
         def product(r):
             rows = slice(r * P, (r + 1) * P)
-            acc = acc_pool.tile([P, 512], F32, name="acc")
+            acc = acc_pool.tile([P, 512], F32, name="acc", tag="bank%d" % (1, 2, 3, 5)[r])
             nc.tensor.matmul_mx(out=acc[:], lhsT=vcode[:, rows].bitcast(FP8X4), lhsT_scale=vscale[:, rows],
                                 rhs=gcode[:].bitcast(FP8X4), rhs_scale=gscale[:], start=True, stop=True)
             return acc

@@ -28,7 +28,7 @@ def tile_attend_tab_looked_changes_pl_kernel(tc, keys_words, keys_scales, notes,
     with ExitStack() as ctx:
         sb = ctx.enter_context(tc.tile_pool(name="sb", bufs=1))
         acc_pool = ctx.enter_context(tc.psum_pool(name="acc", bufs=1))
-        turn_pool = ctx.enter_context(tc.psum_pool(name="turn", bufs=2))
+        turn_pool = ctx.enter_context(tc.psum_pool(name="turn", bufs=1))
 
         def tile(shape, dtype, name, tag=None):
             return sb.tile(shape, dtype, name=name, tag=tag or name, align_bytes=64)
@@ -143,20 +143,26 @@ def tile_attend_tab_looked_changes_pl_kernel(tc, keys_words, keys_scales, notes,
         def relu(t):
             nc.vector.tensor_scalar(gr[:, t, :], g9[t][:], 0.0, rf[:, t : t + 1], ALU.max, ALU.mult)
 
-        turned = []
+        turned = {}
 
         def values(r):
             nc.scalar.activation(vg[r][:], vraw[r][:].indirect(o1[:]), COPY)
             words = vg[r][:].bitcast(F32)
-            if r % 2 == 0:
-                turned.append(turn_pool.tile([P, 2, 2, P], F32, name="ps"))
+            if r == 0:
+                turned[0] = turn_pool.tile([P, 2, 2, P], F32, name="ps", tag="turn0")
+                turned[1] = turned[0]
+            elif r > 1:
+                turned[r] = turn_pool.tile([P, 2, 2, P], F32, name="ps", tag="turn%d" % ((r + 1) % 2))
             for u in range(2):
-                nc.tensor.transpose(turned[r // 2][:, r % 2, u, :], words[:, u : 2 * P : 2], ident[:])
+                nc.tensor.transpose(turned[r][:, r % 2, u, :], words[:, u : 2 * P : 2], ident[:])
 
-        def empty_values(rp):
-            vt.append(tile([P, 2 * P, 4], BF16, "vt%d" % rp, ("vraw2", "y")[rp]))
-            nc.scalar.copy(vt[rp][:].rearrange("p e t -> p (e t)").bitcast(F32).rearrange("p (r e u) -> p r e u", r=2, u=2),
-                           turned[rp][:].rearrange("p r u e -> p r e u"))
+        def empty_values(lo, hi):
+            rp = lo // 2
+            if lo % 2 == 0:
+                vt.append(tile([P, 2 * P, 4], BF16, "vt%d" % rp, ("vraw2", "vraw3")[rp]))
+            rows = slice(lo % 2, hi - 2 * rp)
+            dst = vt[rp][:].rearrange("p e t -> p (e t)").bitcast(F32).rearrange("p (r e u) -> p r e u", r=2, u=2)
+            nc.scalar.copy(dst[:, rows], turned[lo][:, rows].rearrange("p r u e -> p r e u"))
 
         def quant_values(rp):
             cols = slice(rp * 2 * P, (rp + 1) * 2 * P)
@@ -169,10 +175,12 @@ def tile_attend_tab_looked_changes_pl_kernel(tc, keys_words, keys_scales, notes,
             if t > 0:
                 relu(t - 1)
         relu(3)
-        for r in range(4):
+        for r in range(3):
             values(r)
-            if r >= 2:
-                empty_values(r - 2)
+        empty_values(0, 2)
+        values(3)
+        empty_values(2, 3)
+        empty_values(3, 4)
 
         gi = [tile([P, JH, 4], BF16, "gi%d" % h) for h in range(2)]
         gcode = tile([P, J], U32, "gcode")
@@ -210,13 +218,15 @@ def tile_attend_tab_looked_changes_pl_kernel(tc, keys_words, keys_scales, notes,
         damp(1, accs[1])
         quant_values(1)
         accs.extend([product(2), product(3)])
-        y = tile([P, 4, J], F32, "y")
+        y = tile([P, 4, J], F32, "y", "vraw3")
         finish(0, accs[0])
         finish(1, accs[1])
         damp(2, accs[2])
         damp(3, accs[3])
         finish(2, accs[2])
-        finish(3, accs[3])
+        for lo in (JH, 0):
+            nc.vector.tensor_tensor(y[:, 3, lo : lo + JH], accs[3][:, lo : lo + JH], tmp[:, 3, PAD - 1 + lo : PAD - 1 + lo + JH], ALU.subtract)
+        nc.sync.dma_start(oview[:, 3, :], y[:, 3, :])
         for h in range(2):
             dst, src = weave(yb[h][:], y[:, :, h * JH : (h + 1) * JH])
             if h == 0:

from contextlib import ExitStack

import concourse.mybir as mybir
from concourse.masks import make_identity

F32 = mybir.dt.float32
BF16 = mybir.dt.bfloat16
I32 = mybir.dt.int32
U32 = mybir.dt.uint32
U16 = mybir.dt.uint16
U8 = mybir.dt.uint8
FP8X4 = mybir.dt.float8_e4m3fn_x4
FP4X4 = mybir.dt.float4_e2m1fn_x4
ALU = mybir.AluOpType
COPY = mybir.ActivationFunctionType.Copy

P = 128
D, T, I, J, U, E = 512, 2048, 512, 512, 1024, 512
FLOPS = 2 * D * I * U + 2 * I * E * J
NC = 4
CW = U // NC
JH = J // 2
PAD = 8


def tile_attend_tab_looked_changes_pl_kernel(tc, keys_words, keys_scales, notes, rowf, vals, mem, offs, offs2, offs3, out_0, out_1, out_2):
    nc = tc.nc
    with ExitStack() as ctx:
        sb = ctx.enter_context(tc.tile_pool(name="sb", bufs=1))
        acc_pool = ctx.enter_context(tc.psum_pool(name="acc", bufs=1))
        turn_pool = ctx.enter_context(tc.psum_pool(name="turn", bufs=1))

        def tile(shape, dtype, name, tag=None):
            return sb.tile(shape, dtype, name=name, tag=tag or name, align_bytes=64)

        o1 = tile([P, 32], U16, "o1")
        o2 = tile([P, 32], U16, "o2")
        o3 = tile([P, 32], U16, "o3")
        kw = tile([P, T], U16, "kw")
        ks = tile([P, T], U8, "ks")
        nraw = [tile([P, 4, CW], F32, "nraw%d" % c) for c in range(NC)]
        vraw = [tile([P, T], F32, "vraw%d" % r) for r in range(4)]
        rf = tile([P, 4], F32, "rf")
        mb = tile([P, J], F32, "mb")
        tmp = tile([P, 4, PAD + J], F32, "tmp")
        ident = tile([P, P], F32, "ident")

        nc.vector.memset(ks[:].bitcast(I32), 0)
        nc.vector.memset(tmp[:, :, PAD - 1 : PAD], 0.0)
        make_identity(nc, ident[:])

        nc.sync.dma_start(o1[:], offs)
        nc.sync.dma_start(kw[:].bitcast(I32), keys_words[0].bitcast(I32))
        for q in range(4):
            nc.sync.dma_start(ks[32 * q : 32 * q + 4, :].bitcast(I32), keys_scales[0, 4 * q : 4 * q + 4, :].bitcast(I32))
        nview = notes.rearrange("(p t) u -> p t u", t=4)
        for c in range(NC):
            nc.sync.dma_start(nraw[c][:], nview[:, :, c * CW : (c + 1) * CW])
            if c == 1:
                nc.sync.dma_start(o3[:], offs3)
                nc.sync.dma_start(o2[:], offs2)
        nc.sync.dma_start(rf[:], rowf.rearrange("(p t) o -> p (t o)", t=4))
        vview = vals.rearrange("(m r) t -> r m t", r=4)
        for r in range(4):
            nc.sync.dma_start(vraw[r][:], vview[r])
            if r == 1:
                nc.sync.dma_start(mb[:], mem[0].partition_broadcast(P))

        kg = tile([P, I], U16, "kg")
        kd = tile([P, I], U16, "kd")
        ksd = tile([P, I], U8, "ksd")
        nc.vector.tensor_copy(kg[:], kw[:].indirect(o1[:]))
        nc.vector.tensor_copy(ksd[:].rearrange("p (t m) -> p m t", t=4), ks[:].indirect(o1[:]))
        nc.vector.tensor_copy(kd[:].rearrange("p (t m) -> p t m", t=4), kg[:].rearrange("p (m t) -> p t m", t=4))

        ncode = tile([P, U], U32, "ncode")
        nscale = tile([P, U], U8, "nscale")
        nb = [tile([P, CW, 4], BF16, "nb0"), tile([P, CW, 4], BF16, "nb1"), tile([P, 2 * CW, 4], BF16, "nb3")]

        def weave(dst, src):
            return dst.rearrange("p (c i) t -> p c t i", i=4), src.rearrange("p t (c i) -> p c t i", i=4)

        def cast_notes(c):
            dst, src = weave(nb[c][:] if c < 2 else nb[2][:, (c - 2) * CW : (c - 1) * CW, :], nraw[c][:])
            if c < 3:
                nc.scalar.activation(dst, src, COPY)
            else:
                nc.vector.tensor_copy(dst, src)

        def quant_notes(c):
            cols = slice(c * CW, (c + 1) * CW if c < 2 else U)
            nc.vector.quantize_mx(out=ncode[:, cols].bitcast(FP8X4), scales=nscale[:, cols], in_=nb[c][:].rearrange("p c t -> p (c t)"))

        g1 = {}

        banks = {}

        def wide(t, lo, hi):
            h = lo // 512
            if lo % 512 == 0:
                banks[t, h] = acc_pool.tile([P, 512], F32, name="acc", tag="bank%d" % ((0, 1, 2, 3), (4, 5, 0, 4))[h][t])
            rows = slice(t * P, (t + 1) * P)
            nc.tensor.matmul_mx(out=banks[t, h][:, lo - h * 512 : hi - h * 512], lhsT=kd[:, rows].bitcast(FP4X4), lhsT_scale=ksd[:, rows],
                                rhs=ncode[:, lo:hi].bitcast(FP8X4), rhs_scale=nscale[:, lo:hi], start=True, stop=True)

        def empty(t, h):
            if h == 0:
                g1[t] = tile([P, U], F32, "g1_%d" % t, {2: "nraw3", 3: "nb3"}.get(t))
            dst = g1[t][:, h * 512 : (h + 1) * 512]
            if (t, h) in ((2, 0), (3, 0), (1, 1), (2, 1)):
                nc.vector.tensor_copy(dst, banks[t, h][:])
            else:
                nc.scalar.copy(dst, banks[t, h][:])

        for c in range(NC):
            cast_notes(c)
            if c != 2:
                quant_notes(min(c, 2))
            if c < 2:
                for t in range(4):
                    wide(t, c * CW, (c + 1) * CW)
                    if c == 1 and t < 2:
                        empty(t, 0)
        for t in range(2, 4):
            empty(t, 0)
        for t in range(4):
            wide(t, 512, U)
        for t in range(3):
            empty(t, 1)

        gb = [tile([P, J], F32, "gb%d" % t) for t in range(4)]
        g9 = [tile([P, J], F32, "g9_%d" % t) for t in range(4)]
        gr = tile([P, 4, J], BF16, "gr")
        vg = [tile([P, I], BF16, "vg%d" % r) for r in range(4)]
        vt = []
        vcode = tile([P, E], U32, "vcode")
        vscale = tile([P, E], U8, "vscale")

        def table(t):
            nc.scalar.activation(gb[t][:], g1[t][:].indirect(o3[:]), COPY)
            nc.vector.tensor_tensor(g9[t][:], g1[t][:].indirect(o2[:]), gb[t][:], ALU.subtract)

        def relu(t):
            nc.vector.tensor_scalar(gr[:, t, :], g9[t][:], 0.0, rf[:, t : t + 1], ALU.max, ALU.mult)

        turned = {}

        def values(r):
            nc.scalar.activation(vg[r][:], vraw[r][:].indirect(o1[:]), COPY)
            words = vg[r][:].bitcast(F32)
            if r == 0:
                turned[0] = turn_pool.tile([P, 2, 2, P], F32, name="ps", tag="turn0")
                turned[1] = turned[0]
            elif r > 1:
                turned[r] = turn_pool.tile([P, 2, 2, P], F32, name="ps", tag="turn%d" % ((r + 1) % 2))
            for u in range(2):
                nc.tensor.transpose(turned[r][:, r % 2, u, :], words[:, u : 2 * P : 2], ident[:])

        def empty_values(lo, hi):
            rp = lo // 2
            if lo % 2 == 0:
                vt.append(tile([P, 2 * P, 4], BF16, "vt%d" % rp, ("vraw2", "vraw3")[rp]))
            rows = slice(lo % 2, hi - 2 * rp)
            dst = vt[rp][:].rearrange("p e t -> p (e t)").bitcast(F32).rearrange("p (r e u) -> p r e u", r=2, u=2)
            nc.scalar.copy(dst[:, rows], turned[lo][:, rows].rearrange("p r u e -> p r e u"))

        def quant_values(rp):
            cols = slice(rp * 2 * P, (rp + 1) * 2 * P)
            nc.vector.quantize_mx(out=vcode[:, cols].bitcast(FP8X4), scales=vscale[:, cols], in_=vt[rp][:].rearrange("p e t -> p (e t)"))

        for t in range(4):
            if t == 1:
                empty(3, 1)
            table(t)
            if t > 0:
                relu(t - 1)
        relu(3)
        for r in range(3):
            values(r)
        empty_values(0, 2)
        values(3)
        empty_values(2, 3)
        empty_values(3, 4)

        gi = [tile([P, JH, 4], BF16, "gi%d" % h) for h in range(2)]
        gcode = tile([P, J], U32, "gcode")
        gscale = tile([P, J], U8, "gscale")
        for h in range(2):
            dst, src = weave(gi[h][:], gr[:, :, h * JH : (h + 1) * JH])
            nc.vector.tensor_copy(dst, src)
        for h in range(2):
            cols = slice(h * JH, (h + 1) * JH)
            nc.vector.quantize_mx(out=gcode[:, cols].bitcast(FP8X4), scales=gscale[:, cols], in_=gi[h][:].rearrange("p c t -> p (c t)"))

        yb = [tile([P, JH, 4], BF16, "yb%d" % h) for h in range(2)]
        ycode = tile([P, J], U32, "ycode")
        yscale = tile([P, J], U8, "yscale")
        oview = out_0.rearrange("(p r) j -> p r j", r=4)
        cview = out_1[0].rearrange("p c r -> p (c r)").bitcast(I32)

        def product(r):
            rows = slice(r * P, (r + 1) * P)
            acc = acc_pool.tile([P, 512], F32, name="acc", tag="bank%d" % (1, 2, 3, 5)[r])
            nc.tensor.matmul_mx(out=acc[:], lhsT=vcode[:, rows].bitcast(FP8X4), lhsT_scale=vscale[:, rows],
                                rhs=gcode[:].bitcast(FP8X4), rhs_scale=gscale[:], start=True, stop=True)
            return acc

        def damp(r, acc):
            nc.vector.tensor_tensor(tmp[:, r, PAD : PAD + J - 1], acc[:, 0 : J - 1], mb[:, 1:J], ALU.mult)

        def finish(r, acc):
            nc.vector.tensor_tensor(y[:, r, :], acc[:], tmp[:, r, PAD - 1 : PAD - 1 + J], ALU.subtract)
            nc.sync.dma_start(oview[:, r, :], y[:, r, :])

        quant_values(0)
        accs = [product(0), product(1)]
        damp(0, accs[0])
        damp(1, accs[1])
        quant_values(1)
        accs.extend([product(2), product(3)])
        y = tile([P, 4, J], F32, "y", "vraw3")
        finish(0, accs[0])
        finish(1, accs[1])
        damp(2, accs[2])
        damp(3, accs[3])
        finish(2, accs[2])
        for lo in (JH, 0):
            nc.vector.tensor_tensor(y[:, 3, lo : lo + JH], accs[3][:, lo : lo + JH], tmp[:, 3, PAD - 1 + lo : PAD - 1 + lo + JH], ALU.subtract)
        nc.sync.dma_start(oview[:, 3, :], y[:, 3, :])
        for h in range(2):
            dst, src = weave(yb[h][:], y[:, :, h * JH : (h + 1) * JH])
            if h == 0:
                nc.vector.tensor_copy(dst, src)
            else:
                nc.scalar.copy(dst, src)
        for h in range(2):
            cols = slice(h * JH, (h + 1) * JH)
            nc.vector.quantize_mx(out=ycode[:, cols].bitcast(FP8X4), scales=yscale[:, cols], in_=yb[h][:].rearrange("p c t -> p (c t)"))
            nc.sync.dma_start(cview[:, cols], ycode[:, cols].bitcast(I32))
        for q in range(4):
            eng = nc.sync if q % 2 else nc.scalar
            eng.dma_start(out_2[0, 4 * q : 4 * q + 4, :].bitcast(I32), yscale[32 * q : 32 * q + 4, :].bitcast(I32))
